import numpy as np
import ml_dtypes


def mxq(x, axis, fmt="e4m3"):
    dtype, down = {"e4m3": (ml_dtypes.float8_e4m3fn, 7), "e5m2": (ml_dtypes.float8_e5m2, 14)}[fmt]
    v = np.moveaxis(np.asarray(x, np.float32).astype(ml_dtypes.bfloat16).astype(np.float64), axis, -1)
    blocks = v.reshape(v.shape[:-1] + (-1, 32))
    amax = np.abs(blocks).max(-1, keepdims=True)
    byte = np.maximum(np.where(amax > 0, np.frexp(amax)[1] - 1 + 127, 0) - down, 1)
    scale = np.exp2(byte - 127.0)
    codes = (blocks / scale).astype(np.float32).astype(dtype).astype(np.float64)
    return np.moveaxis((codes * scale).reshape(v.shape), -1, axis)


WIDE = False


def mx_kscale(k):
    if not WIDE:
        return np.ones(k)
    levels = np.array([10, -10, 5, -5, 0])
    if k % 512:
        return np.exp2(np.random.permutation(np.resize(levels, k // 32))).repeat(32)
    a = np.empty((k // 512, 16))
    for p in range(k // 512):
        a[p, :8] = np.random.permutation(np.resize(levels, 8))
        for g in range(8):
            far = levels[np.abs(levels - a[p, g]) >= 10]
            a[p, g + 8] = far[np.random.randint(len(far))]
    return np.exp2(a.ravel()).repeat(32)


def f64(x):
    return np.asarray(x).astype(np.float64)


def striped(idx):
    return np.tile(idx.reshape(-1, 16).T, (8, 1)).astype(np.uint16)


def unstriped(offs):
    return offs[:16].T.reshape(-1).astype(np.int64)


def silu(v):
    return v / (1.0 + np.exp(-np.maximum(v, -700.0)))


K, T, S, V, H, N = 512, 1024, 512, 1024, 512, 256
P = 2 ** 7


def setup_inputs():
    n = np.random.standard_normal
    s = mx_kscale(K)[:, None]
    u = mx_kscale(H)
    return {
        "xT": (n((K, T)) * s).astype(np.float32),
        "w1": (n((K, H)) / np.sqrt(K) / s * u).astype(np.float32),
        "w2": (n((H, N)) / np.sqrt(H) / u[:, None]).astype(np.float32),
        "gate": np.tile(np.random.uniform(0.5, 1.5, S), (P, 1)).astype(np.float32),
        "offs": striped(np.random.permutation(T)[:S]),
        "pos1": striped(np.random.permutation(V)[:S]),
    }


def reference(xT, w1, w2, gate, offs, pos1):
    h = silu(mxq(f64(w1), 0, "e4m3").T @ mxq(f64(xT)[:, unstriped(offs)], 0, "e4m3"))
    z = np.zeros((H, V))
    z[:, unstriped(pos1)] = f64(gate)[:1] * h
    return mxq(f64(w2), 0, "e4m3").T @ mxq(z, 0, "e4m3")

@@ -1,0 +1,176 @@
+from contextlib import ExitStack
+
+import concourse.mybir as mybir
+
+K, T, S, V, H, N = 512, 1024, 512, 1024, 512, 256
+FLOPS = 2 * K * H * S + 2 * H * N * V
+
+F32 = mybir.dt.float32
+BF16 = mybir.dt.bfloat16
+U32 = mybir.dt.uint32
+U16 = mybir.dt.uint16
+U8 = mybir.dt.uint8
+FP8X4 = mybir.dt.float8_e4m3fn_x4
+SILU = mybir.ActivationFunctionType.Silu
+MULT = mybir.AluOpType.mult
+
+P = 128
+HALF = 256
+
+
+def tile_picked_voxel_silu_e_kernel(tc, xT, w1, w2, gate, offs, pos1, out):
+    nc = tc.nc
+    with ExitStack() as ctx:
+        held = ctx.enter_context(tc.tile_pool(name="held", bufs=1))
+        psum = ctx.enter_context(tc.psum_pool(name="psum", bufs=8))
+
+        x_rows = xT.rearrange("(p j) t -> p j t", j=4)
+        w1_rows = w1.rearrange("(p j) c -> p j c", j=4)
+        w2_rows = w2.rearrange("(p j) c -> p j c", j=4)
+
+        offs_sb = held.tile([P, S // 16], U16, name="offs_sb")
+        pos_sb = held.tile([P, S // 16], U16, name="pos_sb")
+        x_raw = {}
+        for u in range(2):
+            for b in range(2):
+                t = held.tile([P, 2, T // 2], F32, name=f"x_raw{u}{b}")
+                nc.sync.dma_start(out=t[:], in_=x_rows[:, 2 * u : 2 * u + 2, b * 512 : (b + 1) * 512])
+                x_raw[u, b] = t
+                if u == 0 and b == 0:
+                    nc.sync.dma_start(offs_sb[:], offs)
+        w1_raw = []
+        for u in range(2):
+            t = held.tile([P, 2, H], F32, name=f"w1_raw{u}")
+            nc.sync.dma_start(out=t[:], in_=w1_rows[:, 2 * u : 2 * u + 2, :])
+            w1_raw.append(t)
+        gate_sb = held.tile([P, S], F32, name="gate_sb")
+        nc.sync.dma_start(out=gate_sb[:], in_=gate)
+        nc.sync.dma_start(pos_sb[:], pos1)
+        w2_raw = held.tile([P, 4, N], F32, name="w2_raw")
+        nc.sync.dma_start(out=w2_raw[:], in_=w2_rows)
+
+        warm = held.tile([P, 1], F32, name="warm")
+        warm_out = held.tile([P, 1], F32, name="warm_out")
+        nc.vector.memset(warm[:], 0.0)
+        nc.scalar.activation(warm_out[:], warm[:], SILU)
+
+        z = []
+        for t in range(4):
+            zt = held.tile([P, V], F32, name=f"z{t}")
+            nc.vector.memset(zt[:], 0.0)
+            z.append(zt)
+
+        picked = held.tile([P, S, 4], BF16, name="picked", align_bytes=64)
+        picked_words = picked[:].rearrange("p s j -> p (s j)").bitcast(U32).rearrange("p (s u) -> p s u", u=2)
+        for u in range(2):
+            pairs = held.tile([P, T, 2], BF16, name=f"pairs{u}", align_bytes=64)
+            for b in range(2):
+                cast = nc.vector.tensor_copy if b else nc.scalar.copy
+                cast(out=pairs[:, b * 512 : (b + 1) * 512, :], in_=x_raw[u, b][:].rearrange("p e t -> p t e"))
+            window = pairs[:].rearrange("p t e -> p (t e)").bitcast(U32)
+            for b in range(2):
+                nc.vector.tensor_copy(
+                    out=picked_words[:, b * HALF : (b + 1) * HALF, u],
+                    in_=window.indirect(offs_sb[:, b * 16 : (b + 1) * 16]),
+                )
+        xq = held.tile([P, S], U32, name="xq", align_bytes=64)
+        xs = held.tile([P, S], U8, name="xs", align_bytes=64)
+        for b in range(2):
+            cols = slice(b * HALF, (b + 1) * HALF)
+            nc.vector.quantize_mx(
+                out=xq[:, cols].bitcast(FP8X4),
+                scales=xs[:, cols],
+                in_=picked[:, cols, :].rearrange("p s j -> p (s j)"),
+            )
+
+        w1_cols = []
+        for u in range(2):
+            w1_cols.append(w1_raw[u][:].rearrange("p e (m t) -> p t m e", t=4))
+        w1q, w1s = [], []
+        w1_grouped = []
+        for t in range(4):
+            grouped = held.tile([P, 128, 4], BF16, name=f"w1_grouped{t}", align_bytes=64)
+            nc.scalar.copy(out=grouped[:, :, 0:2], in_=w1_cols[0][:, t])
+            w1_grouped.append(grouped)
+        for t in range(4):
+            nc.vector.tensor_copy(out=w1_grouped[t][:, :, 2:4], in_=w1_cols[1][:, t])
+            q = held.tile([P, 128], U32, name=f"w1q{t}", align_bytes=64)
+            s = held.tile([P, 128], U8, name=f"w1s{t}", align_bytes=64)
+            nc.vector.quantize_mx(
+                out=q[:].bitcast(FP8X4), scales=s[:], in_=w1_grouped[t][:].rearrange("p m j -> p (m j)")
+            )
+            w1q.append(q)
+            w1s.append(s)
+
+        def first_layer(t, cols):
+            bank = psum.tile([P, 512], F32, name="bank")
+            n = cols.stop - cols.start
+            nc.tensor.matmul_mx(
+                out=bank[:, 0:n],
+                lhsT=w1q[t][:].bitcast(FP8X4),
+                lhsT_scale=w1s[t][:],
+                rhs=xq[:, cols].bitcast(FP8X4),
+                rhs_scale=xs[:, cols],
+                start=True,
+                stop=True,
+            )
+            h = held.tile([P, n], F32, name=f"h{t}_{cols.start}")
+            nc.scalar.activation(h[:], bank[:, 0:n], SILU)
+            nc.vector.tensor_tensor(
+                z[t][:].indirect(pos_sb[:, cols.start // 16 : cols.stop // 16]), h[:], gate_sb[:, cols], MULT
+            )
+
+        zi = held.tile([P, V, 4], BF16, name="zi", align_bytes=64)
+        first_layer(0, slice(0, HALF))
+        first_layer(0, slice(HALF, S))
+        for t in range(1, 4):
+            first_layer(t, slice(0, S))
+            if t == 1:
+                w2_grouped = held.tile([P, N, 4], BF16, name="w2_grouped", align_bytes=64)
+                nc.scalar.copy(out=w2_grouped[:], in_=w2_raw[:].rearrange("p j m -> p m j"))
+                w2q = held.tile([P, N], U32, name="w2q", align_bytes=64)
+                w2s = held.tile([P, N], U8, name="w2s", align_bytes=64)
+                nc.vector.quantize_mx(
+                    out=w2q[:].bitcast(FP8X4), scales=w2s[:], in_=w2_grouped[:].rearrange("p m j -> p (m j)")
+                )
+        for t in range(2):
+            nc.scalar.copy(out=zi[:, :, t], in_=z[t][:])
+        nc.scalar.copy(out=zi[:, :, 2:4], in_=z[2][:].unsqueeze(2).to_broadcast([P, V, 2]))
+
+        zq = held.tile([P, V], U32, name="zq", align_bytes=64)
+        zs = held.tile([P, V], U8, name="zs", align_bytes=64)
+        chunks = [slice(c * HALF, (c + 1) * HALF) for c in range(4)]
+        for c in (0, 2, 1, 3):
+            copy = nc.vector.tensor_copy if c < 2 else nc.scalar.copy
+            copy(out=zi[:, chunks[c], 3], in_=z[3][:, chunks[c]])
+        for c in range(4):
+            nc.vector.quantize_mx(
+                out=zq[:, chunks[c]].bitcast(FP8X4),
+                scales=zs[:, chunks[c]],
+                in_=zi[:, chunks[c], :].rearrange("p v j -> p (v j)"),
+            )
+        res = {}
+        for half in range(2):
+            for m in range(2):
+                rt = held.tile([P, 512], F32, name=f"res{half}{m}")
+                res[half, m] = rt
+        for c in range(4):
+            for m in range(2):
+                bank = psum.tile([P, 512], F32, name="bank")
+                nc.tensor.matmul_mx(
+                    out=bank[:, 0:HALF],
+                    lhsT=w2q[:, m * P : (m + 1) * P].bitcast(FP8X4),
+                    lhsT_scale=w2s[:, m * P : (m + 1) * P],
+                    rhs=zq[:, chunks[c]].bitcast(FP8X4),
+                    rhs_scale=zs[:, chunks[c]],
+                    start=True,
+                    stop=True,
+                )
+                dst = res[c // 2, m][:, (c % 2) * HALF : (c % 2 + 1) * HALF]
+                copy = nc.scalar.copy if c < 2 else nc.vector.tensor_copy
+                copy(out=dst, in_=bank[:, 0:HALF])
+                if c % 2:
+                    half = c // 2
+                    nc.sync.dma_start(
+                        out=out[m * P : (m + 1) * P, half * 512 : (half + 1) * 512], in_=res[half, m][:]
+                    )

@@ -30,14 +30,13 @@ def tile_picked_voxel_silu_e_kernel(tc, xT, w1, w2, gate, offs, pos1, out):
 
         offs_sb = held.tile([P, S // 16], U16, name="offs_sb")
         pos_sb = held.tile([P, S // 16], U16, name="pos_sb")
-        x_raw = {}
-        for u in range(2):
-            for b in range(2):
-                t = held.tile([P, 2, T // 2], F32, name=f"x_raw{u}{b}")
-                nc.sync.dma_start(out=t[:], in_=x_rows[:, 2 * u : 2 * u + 2, b * 512 : (b + 1) * 512])
-                x_raw[u, b] = t
-                if u == 0 and b == 0:
-                    nc.sync.dma_start(offs_sb[:], offs)
+        x_raw = []
+        for u, a, b in ((0, 0, 1024), (1, 0, 512), (1, 512, 1024)):
+            t = held.tile([P, 2, b - a], F32, name=f"x_raw{u}_{a}")
+            nc.sync.dma_start(out=t[:], in_=x_rows[:, 2 * u : 2 * u + 2, a:b])
+            x_raw.append(t)
+            if u == 0:
+                nc.sync.dma_start(offs_sb[:], offs)
         w1_raw = []
         for u in range(2):
             t = held.tile([P, 2, H], F32, name=f"w1_raw{u}")
@@ -57,16 +56,26 @@ def tile_picked_voxel_silu_e_kernel(tc, xT, w1, w2, gate, offs, pos1, out):
         z = []
         for t in range(4):
             zt = held.tile([P, V], F32, name=f"z{t}")
-            nc.vector.memset(zt[:], 0.0)
+            nc.gpsimd.memset(zt[:], 0.0)
             z.append(zt)
 
         picked = held.tile([P, S, 4], BF16, name="picked", align_bytes=64)
         picked_words = picked[:].rearrange("p s j -> p (s j)").bitcast(U32).rearrange("p (s u) -> p s u", u=2)
+        casts = (
+            (0, 0, 0, 0, 352, nc.scalar.copy),
+            (0, 0, 352, 352, 672, nc.vector.tensor_copy),
+            (1, 1, 0, 0, 512, nc.scalar.copy),
+            (1, 2, 0, 512, 352, nc.vector.tensor_copy),
+            (1, 2, 352, 864, 160, nc.scalar.copy),
+        )
         for u in range(2):
             pairs = held.tile([P, T, 2], BF16, name=f"pairs{u}", align_bytes=64)
-            for b in range(2):
-                cast = nc.vector.tensor_copy if b else nc.scalar.copy
-                cast(out=pairs[:, b * 512 : (b + 1) * 512, :], in_=x_raw[u, b][:].rearrange("p e t -> p t e"))
+            for cu, raw, src, dst, n, cast in casts:
+                if cu == u:
+                    cast(
+                        out=pairs[:, dst : dst + n, :],
+                        in_=x_raw[raw][:, :, src : src + n].rearrange("p e t -> p t e"),
+                    )
             window = pairs[:].rearrange("p t e -> p (t e)").bitcast(U32)
             for b in range(2):
                 nc.vector.tensor_copy(
@@ -86,29 +95,32 @@ def tile_picked_voxel_silu_e_kernel(tc, xT, w1, w2, gate, offs, pos1, out):
         w1_cols = []
         for u in range(2):
             w1_cols.append(w1_raw[u][:].rearrange("p e (m t) -> p t m e", t=4))
-        w1q, w1s = [], []
-        w1_grouped = []
-        for t in range(4):
-            grouped = held.tile([P, 128, 4], BF16, name=f"w1_grouped{t}", align_bytes=64)
-            nc.scalar.copy(out=grouped[:, :, 0:2], in_=w1_cols[0][:, t])
-            w1_grouped.append(grouped)
-        for t in range(4):
-            nc.vector.tensor_copy(out=w1_grouped[t][:, :, 2:4], in_=w1_cols[1][:, t])
-            q = held.tile([P, 128], U32, name=f"w1q{t}", align_bytes=64)
-            s = held.tile([P, 128], U8, name=f"w1s{t}", align_bytes=64)
+        w1_grouped = held.tile([P, 4, 128, 4], BF16, name="w1_grouped", align_bytes=64)
+        w1q = held.tile([P, 4, 128], U32, name="w1q", align_bytes=64)
+        w1s = held.tile([P, 4, 128], U8, name="w1s", align_bytes=64)
+
+        def quantise_w1(t0, t1):
             nc.vector.quantize_mx(
-                out=q[:].bitcast(FP8X4), scales=s[:], in_=w1_grouped[t][:].rearrange("p m j -> p (m j)")
+                out=w1q[:, t0:t1, :].rearrange("p t m -> p (t m)").bitcast(FP8X4),
+                scales=w1s[:, t0:t1, :].rearrange("p t m -> p (t m)"),
+                in_=w1_grouped[:, t0:t1].rearrange("p t m j -> p (t m j)"),
             )
-            w1q.append(q)
-            w1s.append(s)
+
+        def group_w1(t, u, copy):
+            copy(out=w1_grouped[:, t, :, 2 * u : 2 * u + 2], in_=w1_cols[u][:, t])
+
+        for t in range(4):
+            group_w1(t, 0, nc.scalar.copy)
+        group_w1(0, 1, nc.vector.tensor_copy)
+        quantise_w1(0, 1)
 
         def first_layer(t, cols):
             bank = psum.tile([P, 512], F32, name="bank")
             n = cols.stop - cols.start
             nc.tensor.matmul_mx(
                 out=bank[:, 0:n],
-                lhsT=w1q[t][:].bitcast(FP8X4),
-                lhsT_scale=w1s[t][:],
+                lhsT=w1q[:, t, :].bitcast(FP8X4),
+                lhsT_scale=w1s[:, t, :],
                 rhs=xq[:, cols].bitcast(FP8X4),
                 rhs_scale=xs[:, cols],
                 start=True,
@@ -122,8 +134,14 @@ def tile_picked_voxel_silu_e_kernel(tc, xT, w1, w2, gate, offs, pos1, out):
 
         zi = held.tile([P, V, 4], BF16, name="zi", align_bytes=64)
         first_layer(0, slice(0, HALF))
+        group_w1(1, 1, nc.scalar.copy)
         first_layer(0, slice(HALF, S))
+        quantise_w1(1, 2)
+        group_w1(2, 1, nc.scalar.copy)
+        group_w1(3, 1, nc.scalar.copy)
         for t in range(1, 4):
+            if t == 2:
+                quantise_w1(2, 4)
             first_layer(t, slice(0, S))
             if t == 1:
                 w2_grouped = held.tile([P, N, 4], BF16, name="w2_grouped", align_bytes=64)
@@ -135,7 +153,9 @@ def tile_picked_voxel_silu_e_kernel(tc, xT, w1, w2, gate, offs, pos1, out):
                 )
         for t in range(2):
             nc.scalar.copy(out=zi[:, :, t], in_=z[t][:])
-        nc.scalar.copy(out=zi[:, :, 2:4], in_=z[2][:].unsqueeze(2).to_broadcast([P, V, 2]))
+        for half in range(2):
+            cells = slice(half * 512, (half + 1) * 512)
+            nc.scalar.copy(out=zi[:, cells, 2:4], in_=z[2][:, cells].unsqueeze(2).to_broadcast([P, 512, 2]))
 
         zq = held.tile([P, V], U32, name="zq", align_bytes=64)
         zs = held.tile([P, V], U8, name="zs", align_bytes=64)
@@ -149,12 +169,10 @@ def tile_picked_voxel_silu_e_kernel(tc, xT, w1, w2, gate, offs, pos1, out):
                 scales=zs[:, chunks[c]],
                 in_=zi[:, chunks[c], :].rearrange("p v j -> p (v j)"),
             )
-        res = {}
-        for half in range(2):
-            for m in range(2):
-                rt = held.tile([P, 512], F32, name=f"res{half}{m}")
-                res[half, m] = rt
+        out_rows = out.rearrange("(m p) v -> p m v", p=P)
+        copies = {(2, 1): nc.vector.tensor_copy, (2, 0): nc.vector.tensor_copy, (3, 1): nc.vector.tensor_copy}
         for c in range(4):
+            res = held.tile([P, 2, HALF], F32, name=f"res{c}")
             for m in range(2):
                 bank = psum.tile([P, 512], F32, name="bank")
                 nc.tensor.matmul_mx(
@@ -166,11 +184,5 @@ def tile_picked_voxel_silu_e_kernel(tc, xT, w1, w2, gate, offs, pos1, out):
                     start=True,
                     stop=True,
                 )
-                dst = res[c // 2, m][:, (c % 2) * HALF : (c % 2 + 1) * HALF]
-                copy = nc.scalar.copy if c < 2 else nc.vector.tensor_copy
-                copy(out=dst, in_=bank[:, 0:HALF])
-                if c % 2:
-                    half = c // 2
-                    nc.sync.dma_start(
-                        out=out[m * P : (m + 1) * P, half * 512 : (half + 1) * 512], in_=res[half, m][:]
-                    )
+                copies.get((c, m), nc.scalar.copy)(out=res[:, m, :], in_=bank[:, 0:HALF])
+            nc.sync.dma_start(out=out_rows[:, :, chunks[c]], in_=res[:])

@@ -112,7 +112,9 @@ def tile_picked_voxel_silu_e_kernel(tc, xT, w1, w2, gate, offs, pos1, out):
         for t in range(4):
             group_w1(t, 0, nc.scalar.copy)
         group_w1(0, 1, nc.vector.tensor_copy)
+        group_w1(1, 1, nc.vector.tensor_copy)
         quantise_w1(0, 1)
+        quantise_w1(1, 2)
 
         def first_layer(t, cols):
             bank = psum.tile([P, 512], F32, name="bank")
@@ -134,9 +136,7 @@ def tile_picked_voxel_silu_e_kernel(tc, xT, w1, w2, gate, offs, pos1, out):
 
         zi = held.tile([P, V, 4], BF16, name="zi", align_bytes=64)
         first_layer(0, slice(0, HALF))
-        group_w1(1, 1, nc.scalar.copy)
         first_layer(0, slice(HALF, S))
-        quantise_w1(1, 2)
         group_w1(2, 1, nc.scalar.copy)
         group_w1(3, 1, nc.scalar.copy)
         for t in range(1, 4):
@@ -160,18 +160,28 @@ def tile_picked_voxel_silu_e_kernel(tc, xT, w1, w2, gate, offs, pos1, out):
         zq = held.tile([P, V], U32, name="zq", align_bytes=64)
         zs = held.tile([P, V], U8, name="zs", align_bytes=64)
         chunks = [slice(c * HALF, (c + 1) * HALF) for c in range(4)]
-        for c in (0, 2, 1, 3):
-            copy = nc.vector.tensor_copy if c < 2 else nc.scalar.copy
-            copy(out=zi[:, chunks[c], 3], in_=z[3][:, chunks[c]])
-        for c in range(4):
+        def slot3(a, b, copy):
+            copy(out=zi[:, a:b, 3], in_=z[3][:, a:b])
+
+        def quantise_z(c):
             nc.vector.quantize_mx(
                 out=zq[:, chunks[c]].bitcast(FP8X4),
                 scales=zs[:, chunks[c]],
                 in_=zi[:, chunks[c], :].rearrange("p v j -> p (v j)"),
             )
+
+        slot3(0, 256, nc.vector.tensor_copy)
+        slot3(512, 768, nc.scalar.copy)
+        slot3(256, 384, nc.vector.tensor_copy)
+        quantise_z(0)
+        slot3(384, 512, nc.vector.tensor_copy)
+        slot3(768, 1024, nc.scalar.copy)
+        quantise_z(2)
+        quantise_z(1)
+        quantise_z(3)
         out_rows = out.rearrange("(m p) v -> p m v", p=P)
-        copies = {(2, 1): nc.vector.tensor_copy, (2, 0): nc.vector.tensor_copy, (3, 1): nc.vector.tensor_copy}
-        for c in range(4):
+        copies = {(1, 1): nc.vector.tensor_copy, (1, 0): nc.vector.tensor_copy, (3, 1): nc.vector.tensor_copy}
+        for c in (0, 2, 1, 3):
             res = held.tile([P, 2, HALF], F32, name=f"res{c}")
             for m in range(2):
                 bank = psum.tile([P, 512], F32, name="bank")

@@ -172,16 +172,14 @@ def tile_picked_voxel_silu_e_kernel(tc, xT, w1, w2, gate, offs, pos1, out):
 
         slot3(0, 256, nc.vector.tensor_copy)
         slot3(512, 768, nc.scalar.copy)
-        slot3(256, 384, nc.vector.tensor_copy)
-        quantise_z(0)
-        slot3(384, 512, nc.vector.tensor_copy)
         slot3(768, 1024, nc.scalar.copy)
-        quantise_z(2)
+        quantise_z(0)
+        slot3(256, 512, nc.vector.tensor_copy)
         quantise_z(1)
+        quantise_z(2)
         quantise_z(3)
         out_rows = out.rearrange("(m p) v -> p m v", p=P)
-        copies = {(1, 1): nc.vector.tensor_copy, (1, 0): nc.vector.tensor_copy, (3, 1): nc.vector.tensor_copy}
-        for c in (0, 2, 1, 3):
+        for c in range(4):
             res = held.tile([P, 2, HALF], F32, name=f"res{c}")
             for m in range(2):
                 bank = psum.tile([P, 512], F32, name="bank")
@@ -194,5 +192,9 @@ def tile_picked_voxel_silu_e_kernel(tc, xT, w1, w2, gate, offs, pos1, out):
                     start=True,
                     stop=True,
                 )
-                copies.get((c, m), nc.scalar.copy)(out=res[:, m, :], in_=bank[:, 0:HALF])
-            nc.sync.dma_start(out=out_rows[:, :, chunks[c]], in_=res[:])
+                copy = nc.vector.tensor_copy if c == 3 else nc.scalar.copy
+                copy(out=res[:, m, :], in_=bank[:, 0:HALF])
+                if c == 3:
+                    nc.sync.dma_start(out=out_rows[:, m, chunks[c]], in_=res[:, m, :])
+            if c < 3:
+                nc.sync.dma_start(out=out_rows[:, :, chunks[c]], in_=res[:])

from contextlib import ExitStack

import concourse.mybir as mybir

K, T, S, V, H, N = 512, 1024, 512, 1024, 512, 256
FLOPS = 2 * K * H * S + 2 * H * N * V

F32 = mybir.dt.float32
BF16 = mybir.dt.bfloat16
U32 = mybir.dt.uint32
U16 = mybir.dt.uint16
U8 = mybir.dt.uint8
FP8X4 = mybir.dt.float8_e4m3fn_x4
SILU = mybir.ActivationFunctionType.Silu
MULT = mybir.AluOpType.mult

P = 128
HALF = 256


def tile_picked_voxel_silu_e_kernel(tc, xT, w1, w2, gate, offs, pos1, out):
    nc = tc.nc
    with ExitStack() as ctx:
        held = ctx.enter_context(tc.tile_pool(name="held", bufs=1))
        psum = ctx.enter_context(tc.psum_pool(name="psum", bufs=8))

        x_rows = xT.rearrange("(p j) t -> p j t", j=4)
        w1_rows = w1.rearrange("(p j) c -> p j c", j=4)
        w2_rows = w2.rearrange("(p j) c -> p j c", j=4)

        offs_sb = held.tile([P, S // 16], U16, name="offs_sb")
        pos_sb = held.tile([P, S // 16], U16, name="pos_sb")
        x_raw = []
        for u, a, b in ((0, 0, 1024), (1, 0, 512), (1, 512, 1024)):
            t = held.tile([P, 2, b - a], F32, name=f"x_raw{u}_{a}")
            nc.sync.dma_start(out=t[:], in_=x_rows[:, 2 * u : 2 * u + 2, a:b])
            x_raw.append(t)
            if u == 0:
                nc.sync.dma_start(offs_sb[:], offs)
        w1_raw = []
        for u in range(2):
            t = held.tile([P, 2, H], F32, name=f"w1_raw{u}")
            nc.sync.dma_start(out=t[:], in_=w1_rows[:, 2 * u : 2 * u + 2, :])
            w1_raw.append(t)
        gate_sb = held.tile([P, S], F32, name="gate_sb")
        nc.sync.dma_start(out=gate_sb[:], in_=gate)
        nc.sync.dma_start(pos_sb[:], pos1)
        w2_raw = held.tile([P, 4, N], F32, name="w2_raw")
        nc.sync.dma_start(out=w2_raw[:], in_=w2_rows)

        warm = held.tile([P, 1], F32, name="warm")
        warm_out = held.tile([P, 1], F32, name="warm_out")
        nc.vector.memset(warm[:], 0.0)
        nc.scalar.activation(warm_out[:], warm[:], SILU)

        z = []
        for t in range(4):
            zt = held.tile([P, V], F32, name=f"z{t}")
            nc.gpsimd.memset(zt[:], 0.0)
            z.append(zt)

        picked = held.tile([P, S, 4], BF16, name="picked", align_bytes=64)
        picked_words = picked[:].rearrange("p s j -> p (s j)").bitcast(U32).rearrange("p (s u) -> p s u", u=2)
        casts = (
            (0, 0, 0, 0, 352, nc.scalar.copy),
            (0, 0, 352, 352, 672, nc.vector.tensor_copy),
            (1, 1, 0, 0, 512, nc.scalar.copy),
            (1, 2, 0, 512, 352, nc.vector.tensor_copy),
            (1, 2, 352, 864, 160, nc.scalar.copy),
        )
        for u in range(2):
            pairs = held.tile([P, T, 2], BF16, name=f"pairs{u}", align_bytes=64)
            for cu, raw, src, dst, n, cast in casts:
                if cu == u:
                    cast(
                        out=pairs[:, dst : dst + n, :],
                        in_=x_raw[raw][:, :, src : src + n].rearrange("p e t -> p t e"),
                    )
            window = pairs[:].rearrange("p t e -> p (t e)").bitcast(U32)
            for b in range(2):
                nc.vector.tensor_copy(
                    out=picked_words[:, b * HALF : (b + 1) * HALF, u],
                    in_=window.indirect(offs_sb[:, b * 16 : (b + 1) * 16]),
                )
        xq = held.tile([P, S], U32, name="xq", align_bytes=64)
        xs = held.tile([P, S], U8, name="xs", align_bytes=64)
        for b in range(2):
            cols = slice(b * HALF, (b + 1) * HALF)
            nc.vector.quantize_mx(
                out=xq[:, cols].bitcast(FP8X4),
                scales=xs[:, cols],
                in_=picked[:, cols, :].rearrange("p s j -> p (s j)"),
            )

        w1_cols = []
        for u in range(2):
            w1_cols.append(w1_raw[u][:].rearrange("p e (m t) -> p t m e", t=4))
        w1_grouped = held.tile([P, 4, 128, 4], BF16, name="w1_grouped", align_bytes=64)
        w1q = held.tile([P, 4, 128], U32, name="w1q", align_bytes=64)
        w1s = held.tile([P, 4, 128], U8, name="w1s", align_bytes=64)

        def quantise_w1(t0, t1):
            nc.vector.quantize_mx(
                out=w1q[:, t0:t1, :].rearrange("p t m -> p (t m)").bitcast(FP8X4),
                scales=w1s[:, t0:t1, :].rearrange("p t m -> p (t m)"),
                in_=w1_grouped[:, t0:t1].rearrange("p t m j -> p (t m j)"),
            )

        def group_w1(t, u, copy):
            copy(out=w1_grouped[:, t, :, 2 * u : 2 * u + 2], in_=w1_cols[u][:, t])

        for t in range(4):
            group_w1(t, 0, nc.scalar.copy)
        group_w1(0, 1, nc.vector.tensor_copy)
        group_w1(1, 1, nc.vector.tensor_copy)
        quantise_w1(0, 1)
        quantise_w1(1, 2)

        def first_layer(t, cols):
            bank = psum.tile([P, 512], F32, name="bank")
            n = cols.stop - cols.start
            nc.tensor.matmul_mx(
                out=bank[:, 0:n],
                lhsT=w1q[:, t, :].bitcast(FP8X4),
                lhsT_scale=w1s[:, t, :],
                rhs=xq[:, cols].bitcast(FP8X4),
                rhs_scale=xs[:, cols],
                start=True,
                stop=True,
            )
            h = held.tile([P, n], F32, name=f"h{t}_{cols.start}")
            nc.scalar.activation(h[:], bank[:, 0:n], SILU)
            nc.vector.tensor_tensor(
                z[t][:].indirect(pos_sb[:, cols.start // 16 : cols.stop // 16]), h[:], gate_sb[:, cols], MULT
            )

        zi = held.tile([P, V, 4], BF16, name="zi", align_bytes=64)
        first_layer(0, slice(0, HALF))
        first_layer(0, slice(HALF, S))
        group_w1(2, 1, nc.scalar.copy)
        group_w1(3, 1, nc.scalar.copy)
        for t in range(1, 4):
            if t == 2:
                quantise_w1(2, 4)
            first_layer(t, slice(0, S))
            if t == 1:
                w2_grouped = held.tile([P, N, 4], BF16, name="w2_grouped", align_bytes=64)
                nc.scalar.copy(out=w2_grouped[:], in_=w2_raw[:].rearrange("p j m -> p m j"))
                w2q = held.tile([P, N], U32, name="w2q", align_bytes=64)
                w2s = held.tile([P, N], U8, name="w2s", align_bytes=64)
                nc.vector.quantize_mx(
                    out=w2q[:].bitcast(FP8X4), scales=w2s[:], in_=w2_grouped[:].rearrange("p m j -> p (m j)")
                )
        for t in range(2):
            nc.scalar.copy(out=zi[:, :, t], in_=z[t][:])
        for half in range(2):
            cells = slice(half * 512, (half + 1) * 512)
            nc.scalar.copy(out=zi[:, cells, 2:4], in_=z[2][:, cells].unsqueeze(2).to_broadcast([P, 512, 2]))

        zq = held.tile([P, V], U32, name="zq", align_bytes=64)
        zs = held.tile([P, V], U8, name="zs", align_bytes=64)
        chunks = [slice(c * HALF, (c + 1) * HALF) for c in range(4)]
        def slot3(a, b, copy):
            copy(out=zi[:, a:b, 3], in_=z[3][:, a:b])

        def quantise_z(c):
            nc.vector.quantize_mx(
                out=zq[:, chunks[c]].bitcast(FP8X4),
                scales=zs[:, chunks[c]],
                in_=zi[:, chunks[c], :].rearrange("p v j -> p (v j)"),
            )

        slot3(0, 256, nc.vector.tensor_copy)
        slot3(512, 768, nc.scalar.copy)
        slot3(768, 1024, nc.scalar.copy)
        quantise_z(0)
        slot3(256, 512, nc.vector.tensor_copy)
        quantise_z(1)
        quantise_z(2)
        quantise_z(3)
        out_rows = out.rearrange("(m p) v -> p m v", p=P)
        for c in range(4):
            res = held.tile([P, 2, HALF], F32, name=f"res{c}")
            for m in range(2):
                bank = psum.tile([P, 512], F32, name="bank")
                nc.tensor.matmul_mx(
                    out=bank[:, 0:HALF],
                    lhsT=w2q[:, m * P : (m + 1) * P].bitcast(FP8X4),
                    lhsT_scale=w2s[:, m * P : (m + 1) * P],
                    rhs=zq[:, chunks[c]].bitcast(FP8X4),
                    rhs_scale=zs[:, chunks[c]],
                    start=True,
                    stop=True,
                )
                copy = nc.vector.tensor_copy if c == 3 else nc.scalar.copy
                copy(out=res[:, m, :], in_=bank[:, 0:HALF])
                if c == 3:
                    nc.sync.dma_start(out=out_rows[:, m, chunks[c]], in_=res[:, m, :])
            if c < 3:
                nc.sync.dma_start(out=out_rows[:, :, chunks[c]], in_=res[:])
